import numpy as np
import ml_dtypes


def mxq(x, axis, fmt="e4m3"):
    dtype, down = {"e4m3": (ml_dtypes.float8_e4m3fn, 7), "e5m2": (ml_dtypes.float8_e5m2, 14)}[fmt]
    v = np.moveaxis(np.asarray(x, np.float32).astype(ml_dtypes.bfloat16).astype(np.float64), axis, -1)
    blocks = v.reshape(v.shape[:-1] + (-1, 32))
    amax = np.abs(blocks).max(-1, keepdims=True)
    byte = np.maximum(np.where(amax > 0, np.frexp(amax)[1] - 1 + 127, 0) - down, 1)
    scale = np.exp2(byte - 127.0)
    codes = (blocks / scale).astype(np.float32).astype(dtype).astype(np.float64)
    return np.moveaxis((codes * scale).reshape(v.shape), -1, axis)


WIDE = False


def mx_kscale(k):
    if not WIDE:
        return np.ones(k)
    levels = np.array([10, -10, 5, -5, 0])
    if k % 512:
        return np.exp2(np.random.permutation(np.resize(levels, k // 32))).repeat(32)
    a = np.empty((k // 512, 16))
    for p in range(k // 512):
        a[p, :8] = np.random.permutation(np.resize(levels, 8))
        for g in range(8):
            far = levels[np.abs(levels - a[p, g]) >= 10]
            a[p, g + 8] = far[np.random.randint(len(far))]
    return np.exp2(a.ravel()).repeat(32)


def f64(x):
    return np.asarray(x).astype(np.float64)


def striped(idx):
    return np.tile(idx.reshape(-1, 16).T, (8, 1)).astype(np.uint16)


def unstriped(offs):
    return offs[:16].T.reshape(-1).astype(np.int64)


def relu2(v):
    return np.maximum(v, 0.0) ** 2


K, T, E, C, H, N = 512, 3072, 4, 256, 1024, 128


def by_expert(wq, xq):
    return np.concatenate([wq[e].T @ xq[:, e * C:(e + 1) * C] for e in range(E)], axis=1)


def setup_inputs():
    n = np.random.standard_normal
    s = mx_kscale(K)[:, None]
    u = mx_kscale(H)
    return {
        "xT": (n((K, T)) * s).astype(np.float32),
        "w1": (n((E, K, H)) / np.sqrt(K) / s[None] * u[None, None, :]).astype(np.float32),
        "w2": (n((E, H, N)) / np.sqrt(H) / u[None, :, None] ** 2).astype(np.float32),
        "gate": np.tile(np.random.uniform(0.2, 1.0, E * C), (N, 1)).astype(np.float32),
        "offs": striped(np.random.permutation(T)[:E * C]),
    }


def reference(xT, w1, w2, gate, offs):
    idx = unstriped(offs)
    xq = mxq(f64(xT)[:, idx], 0, "e4m3")
    h = relu2(by_expert(mxq(f64(w1), 1, "e4m3"), xq))
    y = by_expert(mxq(f64(w2), 1, "e4m3"), mxq(h, 0, "e4m3"))
    out = np.zeros((N, T))
    out[:, idx] = f64(gate) * y
    return out

@@ -1,0 +1,214 @@
+from contextlib import ExitStack
+
+import concourse.mybir as mybir
+
+K, T, E, C, H, N = 512, 3072, 4, 256, 1024, 128
+P = 128
+SLOTS = E * C
+FLOPS = 2 * SLOTS * H * (K + N)
+
+F32 = mybir.dt.float32
+BF16 = mybir.dt.bfloat16
+U32 = mybir.dt.uint32
+U16 = mybir.dt.uint16
+U8 = mybir.dt.uint8
+FP8X4 = mybir.dt.float8_e4m3fn_x4
+MULT = mybir.AluOpType.mult
+RELU = mybir.ActivationFunctionType.Relu
+SQUARE = mybir.ActivationFunctionType.Square
+
+X_CHUNK = 1024
+X_VECTOR = 704
+W1_VECTOR = 72
+FIRST_SCATTER = 640
+
+
+def tile_routed_moe_kernel(tc, xT, w1, w2, gate, offs, out):
+    nc = tc.nc
+    with ExitStack() as ctx:
+        keep = ctx.enter_context(tc.tile_pool(name="keep", bufs=1))
+        xraw_pool = ctx.enter_context(tc.tile_pool(name="xraw", bufs=4))
+        wraw_pool = ctx.enter_context(tc.tile_pool(name="wraw", bufs=4))
+        work = ctx.enter_context(tc.tile_pool(name="work", bufs=3))
+        hbank = ctx.enter_context(tc.psum_pool(name="hbank", bufs=6))
+        ybank = ctx.enter_context(tc.psum_pool(name="ybank", bufs=2))
+
+        offsets = keep.tile([P, SLOTS // 16], U16, name="offsets")
+        nc.sync.dma_start(offsets[:], offs)
+
+        window = keep.tile([P, T], F32, name="window")
+        nc.vector.memset(window[:], 0.0)
+
+        pairs = [keep.tile([P, T * 2], BF16, name=f"pairs{u}", align_bytes=64) for u in range(2)]
+        grouped = keep.tile([P, SLOTS * 4], BF16, name="grouped", align_bytes=64)
+        grouped_words = grouped[:].bitcast(U32).rearrange("p (n u) -> p n u", u=2)
+        x_codes = keep.tile([P, SLOTS], U32, name="x_codes", align_bytes=64)
+        x_scales = keep.tile([P, SLOTS], U8, name="x_scales", align_bytes=64)
+
+        def gather(u, a, b):
+            nc.vector.tensor_copy(
+                grouped_words[:, a:b, u],
+                pairs[u][:].bitcast(U32).indirect(offsets[:, a // 16 : b // 16]),
+            )
+
+        x_rows = xT.rearrange("(p u j) n -> u p j n", u=2, j=2)
+        for u in range(2):
+            pv = pairs[u][:].rearrange("p (n j) -> p n j", j=2)
+            for c0 in range(0, T, X_CHUNK):
+                raw = xraw_pool.tile([P, 2, X_CHUNK], F32, name="xraw")
+                nc.sync.dma_start(raw[:], x_rows[u, :, :, c0 : c0 + X_CHUNK])
+                rv = raw[:].rearrange("p j n -> p n j")
+                nc.vector.tensor_copy(pv[:, c0 : c0 + X_VECTOR, :], rv[:, :X_VECTOR, :])
+                nc.scalar.copy(pv[:, c0 + X_VECTOR : c0 + X_CHUNK, :], rv[:, X_VECTOR:, :])
+            if u == 0:
+                gather(0, 0, 512)
+                gather(0, 512, 1024)
+
+        w1_raw = {}
+        w2_raw = {}
+
+        def load_w1(s):
+            e, q = divmod(s, 2)
+            raw = wraw_pool.tile([P, 4, 512], F32, name="w1raw")
+            nc.sync.dma_start(raw[:], w1[e].rearrange("(p j) c -> p j c", j=4)[:, :, q * 512 : (q + 1) * 512])
+            w1_raw[s] = raw
+
+        def load_w2(e):
+            raw = wraw_pool.tile([P, 2, 4, N], F32, name="w2raw")
+            nc.sync.dma_start(raw[:], w2[e].rearrange("(q p j) n -> p q j n", q=2, j=4))
+            w2_raw[e] = raw
+
+        gates = keep.tile([P, SLOTS], F32, name="gates")
+        for e in range(E):
+            load_w1(2 * e)
+            if e == E - 1:
+                nc.sync.dma_start(gates[:], gate)
+            load_w1(2 * e + 1)
+            load_w2(e)
+
+        w1_b, w1_q, w2_b, w2_q = {}, {}, {}, {}
+
+        def interleave_w1(s):
+            t = work.tile([P, 2048], BF16, name="w1b", align_bytes=64)
+            ov = t[:].rearrange("p (t m j) -> p m j t", t=4, j=4)
+            iv = w1_raw[s][:].rearrange("p j (m t) -> p m j t", t=4)
+            nc.vector.tensor_copy(ov[:, :W1_VECTOR], iv[:, :W1_VECTOR])
+            nc.scalar.copy(ov[:, W1_VECTOR:], iv[:, W1_VECTOR:])
+            w1_b[s] = t
+
+        def quantize_w1(s):
+            codes = work.tile([P, 512], U32, name="w1c", align_bytes=64)
+            scales = work.tile([P, 512], U8, name="w1s", align_bytes=64)
+            nc.vector.quantize_mx(out=codes[:].bitcast(FP8X4), scales=scales[:], in_=w1_b[s][:])
+            w1_q[s] = (codes, scales)
+
+        def interleave_w2(e):
+            t = work.tile([P, 1024], BF16, name="w2b", align_bytes=64)
+            for q in range(2):
+                ov = t[:, q * 512 : (q + 1) * 512].rearrange("p (c i j) -> p c j i", i=4, j=4)
+                iv = w2_raw[e][:, q].rearrange("p j (c i) -> p c j i", i=4)
+                nc.vector.tensor_copy(ov, iv)
+            w2_b[e] = t
+
+        def quantize_w2(e):
+            codes = work.tile([P, 256], U32, name="w2c", align_bytes=64)
+            scales = work.tile([P, 256], U8, name="w2s", align_bytes=64)
+            nc.vector.quantize_mx(out=codes[:].bitcast(FP8X4), scales=scales[:], in_=w2_b[e][:])
+            w2_q[e] = (codes, scales)
+
+        def quantize_x(a, b):
+            nc.vector.quantize_mx(
+                out=x_codes[:, a:b].bitcast(FP8X4), scales=x_scales[:, a:b], in_=grouped[:, 4 * a : 4 * b]
+            )
+
+        y_sb = keep.tile([P, SLOTS], F32, name="y_sb")
+        y_ps, relus, hbs = {}, {}, {}
+
+        def layer1(s):
+            e = s // 2
+            codes, scales = w1_q[s]
+            r = work.tile([P, C, 4], F32, name="r")
+            for half in range(2):
+                a = e * C + half * 128
+                bank = hbank.tile([P, 4, 128], F32, name="bank")
+                for t in range(4):
+                    nc.tensor.matmul_mx(
+                        out=bank[:, t, :],
+                        lhsT=codes[:, t * 128 : (t + 1) * 128].bitcast(FP8X4),
+                        lhsT_scale=scales[:, t * 128 : (t + 1) * 128],
+                        rhs=x_codes[:, a : a + 128].bitcast(FP8X4),
+                        rhs_scale=x_scales[:, a : a + 128],
+                        start=True,
+                        stop=True,
+                    )
+                rh = r[:, half * 128 : (half + 1) * 128, :]
+                bv = bank[:].rearrange("p t n -> p n t")
+                if s == 7 and half == 1:
+                    nc.vector.tensor_scalar_max(rh, bv, 0.0)
+                else:
+                    nc.scalar.activation(rh, bv, RELU)
+            relus[s] = r
+
+        def square(s):
+            r = relus[s][:].rearrange("p n t -> p (n t)")
+            hb = work.tile([P, C * 4], BF16, name="hb", align_bytes=64)
+            if s == 7:
+                nc.scalar.activation(hb[:, :512], r[:, :512], SQUARE)
+                nc.vector.tensor_tensor(hb[:, 512:], r[:, 512:], r[:, 512:], MULT)
+            else:
+                nc.scalar.activation(hb[:], r, SQUARE)
+            hbs[s] = hb
+
+        def layer2(s):
+            e, q = divmod(s, 2)
+            hc = work.tile([P, C], U32, name="hc", align_bytes=64)
+            hs = work.tile([P, C], U8, name="hs", align_bytes=64)
+            nc.vector.quantize_mx(out=hc[:].bitcast(FP8X4), scales=hs[:], in_=hbs[s][:])
+            if q == 0:
+                y_ps[e] = ybank.tile([P, C], F32, name="y")
+            codes, scales = w2_q[e]
+            nc.tensor.matmul_mx(
+                out=y_ps[e][:],
+                lhsT=codes[:, q * N : (q + 1) * N].bitcast(FP8X4),
+                lhsT_scale=scales[:, q * N : (q + 1) * N],
+                rhs=hc[:].bitcast(FP8X4),
+                rhs_scale=hs[:],
+                start=(q == 0),
+                stop=(q == 1),
+            )
+            if q == 1:
+                nc.scalar.copy(y_sb[:, e * C : (e + 1) * C], y_ps[e][:])
+
+        def scatter(a, b):
+            nc.vector.tensor_tensor(
+                window[:].indirect(offsets[:, a // 16 : b // 16]), y_sb[:, a:b], gates[:, a:b], MULT
+            )
+
+        gather(1, 0, 512)
+        interleave_w1(0)
+        quantize_x(0, 512)
+        interleave_w1(1)
+        quantize_w1(0)
+        gather(1, 512, 1024)
+        for s in range(2 * E):
+            layer1(s)
+            if s + 2 < 2 * E:
+                interleave_w1(s + 2)
+            if s == 0:
+                quantize_x(512, 1024)
+            if s + 1 < 2 * E:
+                quantize_w1(s + 1)
+            if s > 0:
+                square(s - 1)
+            if s % 2 == 0:
+                interleave_w2(s // 2)
+            if s > 0:
+                layer2(s - 1)
+            if s % 2 == 0:
+                quantize_w2(s // 2)
+            if s == 6:
+                scatter(0, FIRST_SCATTER)
+        square(7)
+        layer2(7)
+        scatter(FIRST_SCATTER, SLOTS)
+        nc.sync.dma_start(out, window[:])

@@ -17,19 +17,24 @@ MULT = mybir.AluOpType.mult
 RELU = mybir.ActivationFunctionType.Relu
 SQUARE = mybir.ActivationFunctionType.Square
 
-X_CHUNK = 1024
-X_VECTOR = 704
-W1_VECTOR = 72
+X_CHUNKS = ((1024, 1024, 1024), (1024, 1024, 640, 384))
+FIRST_GATHER = 384
 FIRST_SCATTER = 640
+SCALAR_HALVES = (1,)
+VECTOR_RELUS = ()
+SCALAR_X = ((0, 1024), (1, 0), (1, 1024))
+VECTOR_Y = ()
+SCALAR_W2 = (0,)
 
 
 def tile_routed_moe_kernel(tc, xT, w1, w2, gate, offs, out):
     nc = tc.nc
     with ExitStack() as ctx:
         keep = ctx.enter_context(tc.tile_pool(name="keep", bufs=1))
-        xraw_pool = ctx.enter_context(tc.tile_pool(name="xraw", bufs=4))
-        wraw_pool = ctx.enter_context(tc.tile_pool(name="wraw", bufs=4))
-        work = ctx.enter_context(tc.tile_pool(name="work", bufs=3))
+        xraw_pool = ctx.enter_context(tc.tile_pool(name="xraw", bufs=3))
+        wraw_pool = ctx.enter_context(tc.tile_pool(name="wraw", bufs=5))
+        work = ctx.enter_context(tc.tile_pool(name="work", bufs=4))
+        hwork = ctx.enter_context(tc.tile_pool(name="hwork", bufs=3))
         hbank = ctx.enter_context(tc.psum_pool(name="hbank", bufs=6))
         ybank = ctx.enter_context(tc.psum_pool(name="ybank", bufs=2))
 
@@ -37,7 +42,20 @@ def tile_routed_moe_kernel(tc, xT, w1, w2, gate, offs, out):
         nc.sync.dma_start(offsets[:], offs)
 
         window = keep.tile([P, T], F32, name="window")
-        nc.vector.memset(window[:], 0.0)
+        nc.gpsimd.memset(window[:], 0.0)
+
+        w1_raw, w2_raw, w1_b, w1_q, w2_b, w2_q = {}, {}, {}, {}, {}, {}
+
+        def load_w1(s):
+            e, q = divmod(s, 2)
+            raw = wraw_pool.tile([P, 4, 512], F32, name="w1raw")
+            nc.sync.dma_start(raw[:], w1[e].rearrange("(p j) c -> p j c", j=4)[:, :, q * 512 : (q + 1) * 512])
+            w1_raw[s] = raw
+
+        def load_w2(e):
+            raw = wraw_pool.tile([P, 2, 4, N], F32, name="w2raw")
+            nc.sync.dma_start(raw[:], w2[e].rearrange("(q p j) n -> p q j n", q=2, j=4))
+            w2_raw[e] = raw
 
         pairs = [keep.tile([P, T * 2], BF16, name=f"pairs{u}", align_bytes=64) for u in range(2)]
         grouped = keep.tile([P, SLOTS * 4], BF16, name="grouped", align_bytes=64)
@@ -51,49 +69,14 @@ def tile_routed_moe_kernel(tc, xT, w1, w2, gate, offs, out):
                 pairs[u][:].bitcast(U32).indirect(offsets[:, a // 16 : b // 16]),
             )
 
-        x_rows = xT.rearrange("(p u j) n -> u p j n", u=2, j=2)
-        for u in range(2):
-            pv = pairs[u][:].rearrange("p (n j) -> p n j", j=2)
-            for c0 in range(0, T, X_CHUNK):
-                raw = xraw_pool.tile([P, 2, X_CHUNK], F32, name="xraw")
-                nc.sync.dma_start(raw[:], x_rows[u, :, :, c0 : c0 + X_CHUNK])
-                rv = raw[:].rearrange("p j n -> p n j")
-                nc.vector.tensor_copy(pv[:, c0 : c0 + X_VECTOR, :], rv[:, :X_VECTOR, :])
-                nc.scalar.copy(pv[:, c0 + X_VECTOR : c0 + X_CHUNK, :], rv[:, X_VECTOR:, :])
-            if u == 0:
-                gather(0, 0, 512)
-                gather(0, 512, 1024)
-
-        w1_raw = {}
-        w2_raw = {}
-
-        def load_w1(s):
-            e, q = divmod(s, 2)
-            raw = wraw_pool.tile([P, 4, 512], F32, name="w1raw")
-            nc.sync.dma_start(raw[:], w1[e].rearrange("(p j) c -> p j c", j=4)[:, :, q * 512 : (q + 1) * 512])
-            w1_raw[s] = raw
-
-        def load_w2(e):
-            raw = wraw_pool.tile([P, 2, 4, N], F32, name="w2raw")
-            nc.sync.dma_start(raw[:], w2[e].rearrange("(q p j) n -> p q j n", q=2, j=4))
-            w2_raw[e] = raw
-
-        gates = keep.tile([P, SLOTS], F32, name="gates")
-        for e in range(E):
-            load_w1(2 * e)
-            if e == E - 1:
-                nc.sync.dma_start(gates[:], gate)
-            load_w1(2 * e + 1)
-            load_w2(e)
-
-        w1_b, w1_q, w2_b, w2_q = {}, {}, {}, {}
-
         def interleave_w1(s):
             t = work.tile([P, 2048], BF16, name="w1b", align_bytes=64)
             ov = t[:].rearrange("p (t m j) -> p m j t", t=4, j=4)
             iv = w1_raw[s][:].rearrange("p j (m t) -> p m j t", t=4)
-            nc.vector.tensor_copy(ov[:, :W1_VECTOR], iv[:, :W1_VECTOR])
-            nc.scalar.copy(ov[:, W1_VECTOR:], iv[:, W1_VECTOR:])
+            if s in SCALAR_HALVES:
+                nc.scalar.copy(ov, iv)
+            else:
+                nc.vector.tensor_copy(ov, iv)
             w1_b[s] = t
 
         def quantize_w1(s):
@@ -104,9 +87,11 @@ def tile_routed_moe_kernel(tc, xT, w1, w2, gate, offs, out):
 
         def interleave_w2(e):
             t = work.tile([P, 1024], BF16, name="w2b", align_bytes=64)
-            for q in range(2):
-                ov = t[:, q * 512 : (q + 1) * 512].rearrange("p (c i j) -> p c j i", i=4, j=4)
-                iv = w2_raw[e][:, q].rearrange("p j (c i) -> p c j i", i=4)
+            ov = t[:].rearrange("p (q c i j) -> p q c j i", q=2, i=4, j=4)
+            iv = w2_raw[e][:].rearrange("p q j (c i) -> p q c j i", i=4)
+            if e in SCALAR_W2:
+                nc.scalar.copy(ov, iv)
+            else:
                 nc.vector.tensor_copy(ov, iv)
             w2_b[e] = t
 
@@ -125,9 +110,10 @@ def tile_routed_moe_kernel(tc, xT, w1, w2, gate, offs, out):
         y_ps, relus, hbs = {}, {}, {}
 
         def layer1(s):
-            e = s // 2
+            e, q = divmod(s, 2)
             codes, scales = w1_q[s]
-            r = work.tile([P, C, 4], F32, name="r")
+            if q == 0:
+                relus[e] = hwork.tile([P, 2, C, 4], F32, name="r")
             for half in range(2):
                 a = e * C + half * 128
                 bank = hbank.tile([P, 4, 128], F32, name="bank")
@@ -141,29 +127,26 @@ def tile_routed_moe_kernel(tc, xT, w1, w2, gate, offs, out):
                         start=True,
                         stop=True,
                     )
-                rh = r[:, half * 128 : (half + 1) * 128, :]
+                rh = relus[e][:, q, half * 128 : (half + 1) * 128, :]
                 bv = bank[:].rearrange("p t n -> p n t")
-                if s == 7 and half == 1:
+                if (s, half) in VECTOR_RELUS:
                     nc.vector.tensor_scalar_max(rh, bv, 0.0)
                 else:
                     nc.scalar.activation(rh, bv, RELU)
-            relus[s] = r
 
         def square(s):
-            r = relus[s][:].rearrange("p n t -> p (n t)")
-            hb = work.tile([P, C * 4], BF16, name="hb", align_bytes=64)
-            if s == 7:
-                nc.scalar.activation(hb[:, :512], r[:, :512], SQUARE)
-                nc.vector.tensor_tensor(hb[:, 512:], r[:, 512:], r[:, 512:], MULT)
-            else:
-                nc.scalar.activation(hb[:], r, SQUARE)
-            hbs[s] = hb
+            e, q = divmod(s, 2)
+            if q == 0:
+                hbs[e] = hwork.tile([P, 2, C * 4], BF16, name="hb", align_bytes=64)
+            r = relus[e][:].rearrange("p q n t -> p q (n t)")
+            hb = hbs[e]
+            nc.scalar.activation(hb[:, q], r[:, q], SQUARE)
 
         def layer2(s):
             e, q = divmod(s, 2)
-            hc = work.tile([P, C], U32, name="hc", align_bytes=64)
-            hs = work.tile([P, C], U8, name="hs", align_bytes=64)
-            nc.vector.quantize_mx(out=hc[:].bitcast(FP8X4), scales=hs[:], in_=hbs[s][:])
+            hc = hwork.tile([P, C], U32, name="hc", align_bytes=64)
+            hs = hwork.tile([P, C], U8, name="hs", align_bytes=64)
+            nc.vector.quantize_mx(out=hc[:].bitcast(FP8X4), scales=hs[:], in_=hbs[e][:, q])
             if q == 0:
                 y_ps[e] = ybank.tile([P, C], F32, name="y")
             codes, scales = w2_q[e]
@@ -177,37 +160,69 @@ def tile_routed_moe_kernel(tc, xT, w1, w2, gate, offs, out):
                 stop=(q == 1),
             )
             if q == 1:
-                nc.scalar.copy(y_sb[:, e * C : (e + 1) * C], y_ps[e][:])
+                ys = y_sb[:, e * C : (e + 1) * C]
+                if e in VECTOR_Y:
+                    nc.vector.tensor_copy(ys, y_ps[e][:])
+                else:
+                    nc.scalar.copy(ys, y_ps[e][:])
 
         def scatter(a, b):
             nc.vector.tensor_tensor(
                 window[:].indirect(offsets[:, a // 16 : b // 16]), y_sb[:, a:b], gates[:, a:b], MULT
             )
 
-        gather(1, 0, 512)
+        load_w1(0)
         interleave_w1(0)
-        quantize_x(0, 512)
+        x_rows = xT.rearrange("(p u j) n -> u p j n", u=2, j=2)
+        for u in range(2):
+            pv = pairs[u][:].rearrange("p (n j) -> p n j", j=2)
+            c0 = 0
+            for width in X_CHUNKS[u]:
+                raw = xraw_pool.tile([P, 2, width], F32, name="xraw")
+                nc.sync.dma_start(raw[:], x_rows[u, :, :, c0 : c0 + width])
+                rv = raw[:].rearrange("p j n -> p n j")
+                if (u, c0) in SCALAR_X:
+                    nc.scalar.copy(pv[:, c0 : c0 + width, :], rv)
+                else:
+                    nc.vector.tensor_copy(pv[:, c0 : c0 + width, :], rv)
+                c0 += width
+            if u == 0:
+                quantize_w1(0)
+                gather(0, 0, SLOTS)
+
+        gates = keep.tile([P, SLOTS], F32, name="gates")
+        for e in range(E):
+            if e > 0:
+                load_w1(2 * e)
+            if e == 2:
+                nc.sync.dma_start(gates[:], gate)
+            load_w1(2 * e + 1)
+            load_w2(e)
+
+        gather(1, 0, FIRST_GATHER)
+        quantize_x(0, 256)
         interleave_w1(1)
-        quantize_w1(0)
-        gather(1, 512, 1024)
+        gather(1, FIRST_GATHER, SLOTS)
+        quantize_x(256, 512)
+        quantize_w1(1)
+        quantize_x(512, 1024)
+        interleave_w2(0)
+        quantize_w2(0)
         for s in range(2 * E):
             layer1(s)
+            if s >= 1:
+                square(s - 1)
             if s + 2 < 2 * E:
                 interleave_w1(s + 2)
-            if s == 0:
-                quantize_x(512, 1024)
-            if s + 1 < 2 * E:
-                quantize_w1(s + 1)
-            if s > 0:
-                square(s - 1)
-            if s % 2 == 0:
-                interleave_w2(s // 2)
-            if s > 0:
-                layer2(s - 1)
-            if s % 2 == 0:
-                quantize_w2(s // 2)
-            if s == 6:
-                scatter(0, FIRST_SCATTER)
+            if s >= 2:
+                layer2(s - 2)
+            if s + 2 < 2 * E:
+                quantize_w1(s + 2)
+            if s in (1, 3, 5):
+                interleave_w2((s + 1) // 2)
+                quantize_w2((s + 1) // 2)
+        scatter(0, FIRST_SCATTER)
+        layer2(6)
         square(7)
         layer2(7)
         scatter(FIRST_SCATTER, SLOTS)

from contextlib import ExitStack

import concourse.mybir as mybir

K, T, E, C, H, N = 512, 3072, 4, 256, 1024, 128
P = 128
SLOTS = E * C
FLOPS = 2 * SLOTS * H * (K + N)

F32 = mybir.dt.float32
BF16 = mybir.dt.bfloat16
U32 = mybir.dt.uint32
U16 = mybir.dt.uint16
U8 = mybir.dt.uint8
FP8X4 = mybir.dt.float8_e4m3fn_x4
MULT = mybir.AluOpType.mult
RELU = mybir.ActivationFunctionType.Relu
SQUARE = mybir.ActivationFunctionType.Square

X_CHUNKS = ((1024, 1024, 1024), (1024, 1024, 640, 384))
FIRST_GATHER = 384
FIRST_SCATTER = 640
SCALAR_HALVES = (1,)
VECTOR_RELUS = ()
SCALAR_X = ((0, 1024), (1, 0), (1, 1024))
VECTOR_Y = ()
SCALAR_W2 = (0,)


def tile_routed_moe_kernel(tc, xT, w1, w2, gate, offs, out):
    nc = tc.nc
    with ExitStack() as ctx:
        keep = ctx.enter_context(tc.tile_pool(name="keep", bufs=1))
        xraw_pool = ctx.enter_context(tc.tile_pool(name="xraw", bufs=3))
        wraw_pool = ctx.enter_context(tc.tile_pool(name="wraw", bufs=5))
        work = ctx.enter_context(tc.tile_pool(name="work", bufs=4))
        hwork = ctx.enter_context(tc.tile_pool(name="hwork", bufs=3))
        hbank = ctx.enter_context(tc.psum_pool(name="hbank", bufs=6))
        ybank = ctx.enter_context(tc.psum_pool(name="ybank", bufs=2))

        offsets = keep.tile([P, SLOTS // 16], U16, name="offsets")
        nc.sync.dma_start(offsets[:], offs)

        window = keep.tile([P, T], F32, name="window")
        nc.gpsimd.memset(window[:], 0.0)

        w1_raw, w2_raw, w1_b, w1_q, w2_b, w2_q = {}, {}, {}, {}, {}, {}

        def load_w1(s):
            e, q = divmod(s, 2)
            raw = wraw_pool.tile([P, 4, 512], F32, name="w1raw")
            nc.sync.dma_start(raw[:], w1[e].rearrange("(p j) c -> p j c", j=4)[:, :, q * 512 : (q + 1) * 512])
            w1_raw[s] = raw

        def load_w2(e):
            raw = wraw_pool.tile([P, 2, 4, N], F32, name="w2raw")
            nc.sync.dma_start(raw[:], w2[e].rearrange("(q p j) n -> p q j n", q=2, j=4))
            w2_raw[e] = raw

        pairs = [keep.tile([P, T * 2], BF16, name=f"pairs{u}", align_bytes=64) for u in range(2)]
        grouped = keep.tile([P, SLOTS * 4], BF16, name="grouped", align_bytes=64)
        grouped_words = grouped[:].bitcast(U32).rearrange("p (n u) -> p n u", u=2)
        x_codes = keep.tile([P, SLOTS], U32, name="x_codes", align_bytes=64)
        x_scales = keep.tile([P, SLOTS], U8, name="x_scales", align_bytes=64)

        def gather(u, a, b):
            nc.vector.tensor_copy(
                grouped_words[:, a:b, u],
                pairs[u][:].bitcast(U32).indirect(offsets[:, a // 16 : b // 16]),
            )

        def interleave_w1(s):
            t = work.tile([P, 2048], BF16, name="w1b", align_bytes=64)
            ov = t[:].rearrange("p (t m j) -> p m j t", t=4, j=4)
            iv = w1_raw[s][:].rearrange("p j (m t) -> p m j t", t=4)
            if s in SCALAR_HALVES:
                nc.scalar.copy(ov, iv)
            else:
                nc.vector.tensor_copy(ov, iv)
            w1_b[s] = t

        def quantize_w1(s):
            codes = work.tile([P, 512], U32, name="w1c", align_bytes=64)
            scales = work.tile([P, 512], U8, name="w1s", align_bytes=64)
            nc.vector.quantize_mx(out=codes[:].bitcast(FP8X4), scales=scales[:], in_=w1_b[s][:])
            w1_q[s] = (codes, scales)

        def interleave_w2(e):
            t = work.tile([P, 1024], BF16, name="w2b", align_bytes=64)
            ov = t[:].rearrange("p (q c i j) -> p q c j i", q=2, i=4, j=4)
            iv = w2_raw[e][:].rearrange("p q j (c i) -> p q c j i", i=4)
            if e in SCALAR_W2:
                nc.scalar.copy(ov, iv)
            else:
                nc.vector.tensor_copy(ov, iv)
            w2_b[e] = t

        def quantize_w2(e):
            codes = work.tile([P, 256], U32, name="w2c", align_bytes=64)
            scales = work.tile([P, 256], U8, name="w2s", align_bytes=64)
            nc.vector.quantize_mx(out=codes[:].bitcast(FP8X4), scales=scales[:], in_=w2_b[e][:])
            w2_q[e] = (codes, scales)

        def quantize_x(a, b):
            nc.vector.quantize_mx(
                out=x_codes[:, a:b].bitcast(FP8X4), scales=x_scales[:, a:b], in_=grouped[:, 4 * a : 4 * b]
            )

        y_sb = keep.tile([P, SLOTS], F32, name="y_sb")
        y_ps, relus, hbs = {}, {}, {}

        def layer1(s):
            e, q = divmod(s, 2)
            codes, scales = w1_q[s]
            if q == 0:
                relus[e] = hwork.tile([P, 2, C, 4], F32, name="r")
            for half in range(2):
                a = e * C + half * 128
                bank = hbank.tile([P, 4, 128], F32, name="bank")
                for t in range(4):
                    nc.tensor.matmul_mx(
                        out=bank[:, t, :],
                        lhsT=codes[:, t * 128 : (t + 1) * 128].bitcast(FP8X4),
                        lhsT_scale=scales[:, t * 128 : (t + 1) * 128],
                        rhs=x_codes[:, a : a + 128].bitcast(FP8X4),
                        rhs_scale=x_scales[:, a : a + 128],
                        start=True,
                        stop=True,
                    )
                rh = relus[e][:, q, half * 128 : (half + 1) * 128, :]
                bv = bank[:].rearrange("p t n -> p n t")
                if (s, half) in VECTOR_RELUS:
                    nc.vector.tensor_scalar_max(rh, bv, 0.0)
                else:
                    nc.scalar.activation(rh, bv, RELU)

        def square(s):
            e, q = divmod(s, 2)
            if q == 0:
                hbs[e] = hwork.tile([P, 2, C * 4], BF16, name="hb", align_bytes=64)
            r = relus[e][:].rearrange("p q n t -> p q (n t)")
            hb = hbs[e]
            nc.scalar.activation(hb[:, q], r[:, q], SQUARE)

        def layer2(s):
            e, q = divmod(s, 2)
            hc = hwork.tile([P, C], U32, name="hc", align_bytes=64)
            hs = hwork.tile([P, C], U8, name="hs", align_bytes=64)
            nc.vector.quantize_mx(out=hc[:].bitcast(FP8X4), scales=hs[:], in_=hbs[e][:, q])
            if q == 0:
                y_ps[e] = ybank.tile([P, C], F32, name="y")
            codes, scales = w2_q[e]
            nc.tensor.matmul_mx(
                out=y_ps[e][:],
                lhsT=codes[:, q * N : (q + 1) * N].bitcast(FP8X4),
                lhsT_scale=scales[:, q * N : (q + 1) * N],
                rhs=hc[:].bitcast(FP8X4),
                rhs_scale=hs[:],
                start=(q == 0),
                stop=(q == 1),
            )
            if q == 1:
                ys = y_sb[:, e * C : (e + 1) * C]
                if e in VECTOR_Y:
                    nc.vector.tensor_copy(ys, y_ps[e][:])
                else:
                    nc.scalar.copy(ys, y_ps[e][:])

        def scatter(a, b):
            nc.vector.tensor_tensor(
                window[:].indirect(offsets[:, a // 16 : b // 16]), y_sb[:, a:b], gates[:, a:b], MULT
            )

        load_w1(0)
        interleave_w1(0)
        x_rows = xT.rearrange("(p u j) n -> u p j n", u=2, j=2)
        for u in range(2):
            pv = pairs[u][:].rearrange("p (n j) -> p n j", j=2)
            c0 = 0
            for width in X_CHUNKS[u]:
                raw = xraw_pool.tile([P, 2, width], F32, name="xraw")
                nc.sync.dma_start(raw[:], x_rows[u, :, :, c0 : c0 + width])
                rv = raw[:].rearrange("p j n -> p n j")
                if (u, c0) in SCALAR_X:
                    nc.scalar.copy(pv[:, c0 : c0 + width, :], rv)
                else:
                    nc.vector.tensor_copy(pv[:, c0 : c0 + width, :], rv)
                c0 += width
            if u == 0:
                quantize_w1(0)
                gather(0, 0, SLOTS)

        gates = keep.tile([P, SLOTS], F32, name="gates")
        for e in range(E):
            if e > 0:
                load_w1(2 * e)
            if e == 2:
                nc.sync.dma_start(gates[:], gate)
            load_w1(2 * e + 1)
            load_w2(e)

        gather(1, 0, FIRST_GATHER)
        quantize_x(0, 256)
        interleave_w1(1)
        gather(1, FIRST_GATHER, SLOTS)
        quantize_x(256, 512)
        quantize_w1(1)
        quantize_x(512, 1024)
        interleave_w2(0)
        quantize_w2(0)
        for s in range(2 * E):
            layer1(s)
            if s >= 1:
                square(s - 1)
            if s + 2 < 2 * E:
                interleave_w1(s + 2)
            if s >= 2:
                layer2(s - 2)
            if s + 2 < 2 * E:
                quantize_w1(s + 2)
            if s in (1, 3, 5):
                interleave_w2((s + 1) // 2)
                quantize_w2((s + 1) // 2)
        scatter(0, FIRST_SCATTER)
        layer2(6)
        square(7)
        layer2(7)
        scatter(FIRST_SCATTER, SLOTS)
        nc.sync.dma_start(out, window[:])
